import numpy as np
import ml_dtypes


def mxq(x, axis, fmt="e4m3"):
    dtype, down = {"e4m3": (ml_dtypes.float8_e4m3fn, 7), "e5m2": (ml_dtypes.float8_e5m2, 14)}[fmt]
    v = np.moveaxis(np.asarray(x, np.float32).astype(ml_dtypes.bfloat16).astype(np.float64), axis, -1)
    blocks = v.reshape(v.shape[:-1] + (-1, 32))
    amax = np.abs(blocks).max(-1, keepdims=True)
    byte = np.maximum(np.where(amax > 0, np.frexp(amax)[1] - 1 + 127, 0) - down, 1)
    scale = np.exp2(byte - 127.0)
    codes = (blocks / scale).astype(np.float32).astype(dtype).astype(np.float64)
    return np.moveaxis((codes * scale).reshape(v.shape), -1, axis)


WIDE = False


def mx_kscale(k):
    if not WIDE:
        return np.ones(k)
    levels = np.array([10, -10, 5, -5, 0])
    if k % 512:
        return np.exp2(np.random.permutation(np.resize(levels, k // 32))).repeat(32)
    a = np.empty((k // 512, 16))
    for p in range(k // 512):
        a[p, :8] = np.random.permutation(np.resize(levels, 8))
        for g in range(8):
            far = levels[np.abs(levels - a[p, g]) >= 10]
            a[p, g + 8] = far[np.random.randint(len(far))]
    return np.exp2(a.ravel()).repeat(32)


def f64(x):
    return np.asarray(x).astype(np.float64)


def striped(idx):
    return np.tile(idx.reshape(-1, 16).T, (8, 1)).astype(np.uint16)


def unstriped(offs):
    return offs[:16].T.reshape(-1).astype(np.int64)


def silu(v):
    return v / (1.0 + np.exp(-np.maximum(v, -700.0)))


K, T, E, C, H, N = 1536, 512, 4, 128, 512, 512


def by_expert(wq, xq):
    return np.concatenate([wq[e].T @ xq[:, e * C:(e + 1) * C] for e in range(E)], axis=1)


def setup_inputs():
    n = np.random.standard_normal
    s = mx_kscale(K)[:, None]
    u = mx_kscale(H)
    return {
        "xT": (n((K, T)) * s).astype(np.float32),
        "w1": (n((E, K, H)) / np.sqrt(K) / s[None]).astype(np.float32),
        "w3": (n((E, K, H)) / np.sqrt(K) / s[None] * u[None, None, :]).astype(np.float32),
        "w2": (n((E, H, N)) / np.sqrt(H) / u[None, :, None]).astype(np.float32),
        "gate": np.tile(np.random.uniform(0.2, 1.0, E * C), (N, 1)).astype(np.float32),
        "offs": striped(np.random.permutation(T)[:E * C]),
    }


def reference(xT, w1, w3, w2, gate, offs):
    idx = unstriped(offs)
    xq = mxq(f64(xT)[:, idx], 0, "e4m3")
    h = silu(by_expert(mxq(f64(w1), 1, "e4m3"), xq))
    h = h * by_expert(mxq(f64(w3), 1, "e4m3"), xq)
    y = by_expert(mxq(f64(w2), 1, "e4m3"), mxq(h, 0, "e4m3"))
    out = np.zeros((N, T))
    out[:, idx] = f64(gate) * y
    return out

@@ -1,0 +1,235 @@
+from contextlib import ExitStack
+
+import concourse.mybir as mybir
+
+K, T, E, C, H, N = 1536, 512, 4, 128, 512, 512
+P = 128
+PACK = 4
+K_PASS = P * PACK
+PASSES = K // K_PASS
+
+FLOPS = 2 * E * C * (K * H * 2 + H * N)
+BYTES = 4 * (K * T + 2 * E * K * H + E * H * N + P * E * C + N * T) + 2 * P * E * C // 16
+
+F32 = mybir.dt.float32
+BF16 = mybir.dt.bfloat16
+U32 = mybir.dt.uint32
+U16 = mybir.dt.uint16
+U8 = mybir.dt.uint8
+FP8X4 = mybir.dt.float8_e4m3fn_x4
+MULT = mybir.AluOpType.mult
+SILU = mybir.ActivationFunctionType.Silu
+
+AHEAD = 13
+
+
+def tile_routed_moe_kernel(tc, xT, w1, w3, w2, gate, offs, out):
+    nc = tc.nc
+    with ExitStack() as ctx:
+        keep = ctx.enter_context(tc.tile_pool(name="keep", bufs=1))
+        raws = ctx.enter_context(tc.tile_pool(name="raws", bufs=AHEAD + 1))
+        stage = ctx.enter_context(tc.tile_pool(name="stage", bufs=6))
+        codes = ctx.enter_context(tc.tile_pool(name="codes", bufs=14))
+        small = ctx.enter_context(tc.tile_pool(name="small", bufs=2))
+        psum = ctx.enter_context(tc.psum_pool(name="psum", bufs=2))
+
+        offsets = keep.tile([P, E * C // 16], U16, name="offsets")
+        nc.sync.dma_start(offsets[:], offs)
+
+        warm = keep.tile([P, 1], F32, name="warm")
+        warm_out = keep.tile([P, 1], F32, name="warm_out")
+        nc.vector.memset(warm[:], 0.0)
+        nc.scalar.activation(warm_out[:], warm[:], SILU)
+
+        gate_sb = keep.tile([P, E * C], F32, name="gate_sb")
+        xg_words = keep.tile([P, PASSES, E * C], U32, name="xg_words", align_bytes=64)
+        xg_bytes = keep.tile([P, PASSES, E * C], U8, name="xg_bytes", align_bytes=64)
+        x_words = []
+        x_bytes = []
+        for g in range(PASSES):
+            x_words.append(keep.tile([P, T], U32, name=f"x_words{g}", align_bytes=64))
+            xb = keep.tile([P, T], U8, name=f"x_bytes{g}", align_bytes=64)
+            nc.gpsimd.memset(xb[:], 0)
+            x_bytes.append(xb)
+        windows = []
+        for nb in range(N // P):
+            windows.append(keep.tile([P, T], F32, name=f"window{nb}"))
+
+        chunks = [("x", 0, g, 0, T) for g in range(PASSES)]
+        for e in range(E):
+            for g in range(PASSES):
+                chunks.append(("w1", e, g, 0, H))
+            for g in range(PASSES):
+                chunks.append(("w3", e, g, 0, H))
+            if e < E - 1:
+                chunks.append(("w2", e, 0, 0, N))
+            else:
+                chunks.append(("w2", e, 0, 0, N // 2))
+                chunks.append(("w2", e, 0, N // 2, N))
+
+        raw_of, grouped_of, code_of = {}, {}, {}
+
+        def load(i):
+            if i >= len(chunks):
+                return
+            kind, e, g, c0, c1 = chunks[i]
+            rows = slice(g * K_PASS, (g + 1) * K_PASS)
+            if kind == "x":
+                src = xT[rows, :]
+            elif kind == "w1":
+                src = w1[e, rows, :]
+            elif kind == "w3":
+                src = w3[e, rows, :]
+            else:
+                src = w2[e, :, c0:c1]
+            raw = raws.tile([P, PACK, c1 - c0], F32, name=f"raw{i}", tag="raw")
+            nc.sync.dma_start(out=raw[:], in_=src.rearrange("(p j) w -> p j w", j=PACK))
+            raw_of[i] = raw
+
+        def copy_on(engine, out_, in_):
+            if engine == "v":
+                nc.vector.tensor_copy(out=out_, in_=in_)
+            else:
+                nc.scalar.copy(out_, in_)
+
+        PLAN = {"w1": "svs", "w3": "ssv", "w2": "s"}
+
+        def interleave(i):
+            kind, e, g, c0, c1 = chunks[i]
+            width = c1 - c0
+            raw = raw_of[i]
+            grouped = stage.tile([P, PACK * width], BF16, name=f"grouped{i}", tag="grouped", align_bytes=64)
+            if kind in ("w1", "w3"):
+                dst = grouped[:].rearrange("p (t m j) -> p m j t", t=PACK, j=PACK)
+                src = raw[:].rearrange("p j (m t) -> p m j t", t=PACK)
+            else:
+                dst = grouped[:].rearrange("p (c i j) -> p c j i", i=4, j=PACK)
+                src = raw[:].rearrange("p j (c i) -> p c j i", i=4)
+            n = width // 4
+            if kind == "x":
+                who = "s"
+            elif kind == "w3" and e == E - 1 and g == PASSES - 1:
+                who = "b"
+            elif kind == "w2" and e == E - 1:
+                who = "s" if c0 == 0 else "b"
+            else:
+                who = PLAN[kind][g]
+            if who == "b":
+                cut = (n * 5 // 8) // 8 * 8
+                copy_on("v", dst[:, 0:cut], src[:, 0:cut])
+                copy_on("s", dst[:, cut:n], src[:, cut:n])
+            else:
+                copy_on(who, dst, src)
+            grouped_of[i] = grouped
+
+        def quantize(i):
+            kind, e, g, c0, c1 = chunks[i]
+            if kind == "x":
+                words, scales = x_words[g], x_bytes[g]
+            else:
+                words = codes.tile([P, c1 - c0], U32, name=f"words{i}", tag="words", align_bytes=64)
+                scales = codes.tile([P, c1 - c0], U8, name=f"scales{i}", tag="scales", align_bytes=64)
+            nc.vector.quantize_mx(out=words[:].bitcast(FP8X4), scales=scales[:], in_=grouped_of[i][:])
+            code_of[i] = (words, scales)
+
+        def gather(g):
+            for h in range(2):
+                cols = slice(h * 256, (h + 1) * 256)
+                list_cols = slice(h * 16, (h + 1) * 16)
+                nc.vector.tensor_copy(out=xg_words[:, g, cols], in_=x_words[g][:].indirect(offsets[:, list_cols]))
+                nc.vector.tensor_copy(out=xg_bytes[:, g, cols], in_=x_bytes[g][:].indirect(offsets[:, list_cols]))
+
+        def first_layer(e, ids, tag):
+            acc = psum.tile([P, PACK, C], F32, name=f"{tag}{e}", tag=tag)
+            slots = slice(e * C, (e + 1) * C)
+            for t in range(PACK):
+                cols = slice(t * P, (t + 1) * P)
+                for g in range(PASSES):
+                    words, scales = code_of[ids[g]]
+                    nc.tensor.matmul_mx(
+                        out=acc[:, t, :],
+                        lhsT=words[:, cols].bitcast(FP8X4),
+                        lhsT_scale=scales[:, cols],
+                        rhs=xg_words[:, g, slots].bitcast(FP8X4),
+                        rhs_scale=xg_bytes[:, g, slots],
+                        start=(g == 0),
+                        stop=(g == PASSES - 1),
+                    )
+            return acc
+
+        state = {}
+
+        def after(i):
+            kind, e, g, c0, c1 = chunks[i]
+            slots = slice(e * C, (e + 1) * C)
+            if kind == "x":
+                gather(g)
+            elif kind == "w1" and g == PASSES - 1:
+                acc = first_layer(e, (i - 2, i - 1, i), "a")
+                act = small.tile([P, PACK, C], F32, name=f"act{e}", tag="act")
+                nc.scalar.activation(act[:], acc[:], SILU)
+                state["act"] = act
+            elif kind == "w3" and g == PASSES - 1:
+                acc = first_layer(e, (i - 2, i - 1, i), "b")
+                hid = small.tile([P, C, PACK], BF16, name=f"hid{e}", tag="hid", align_bytes=64)
+                nc.vector.tensor_tensor(
+                    out=hid[:],
+                    in0=acc[:].rearrange("p t c -> p c t"),
+                    in1=state["act"][:].rearrange("p t c -> p c t"),
+                    op=MULT,
+                )
+                h_words = small.tile([P, C], U32, name=f"h_words{e}", tag="h_words", align_bytes=64)
+                h_bytes = small.tile([P, C], U8, name=f"h_bytes{e}", tag="h_bytes", align_bytes=64)
+                nc.vector.quantize_mx(
+                    out=h_words[:].bitcast(FP8X4), scales=h_bytes[:], in_=hid[:].rearrange("p c t -> p (c t)")
+                )
+                state["h"] = (h_words, h_bytes)
+            elif kind == "w2":
+                h_words, h_bytes = state["h"]
+                words, scales = code_of[i]
+                blocks = (c1 - c0) // P
+                acc = psum.tile([P, blocks, C], F32, name=f"y{i}", tag="y")
+                for b in range(blocks):
+                    cols = slice(b * P, (b + 1) * P)
+                    nc.tensor.matmul_mx(
+                        out=acc[:, b, :],
+                        lhsT=words[:, cols].bitcast(FP8X4),
+                        lhsT_scale=scales[:, cols],
+                        rhs=h_words[:].bitcast(FP8X4),
+                        rhs_scale=h_bytes[:],
+                        start=True,
+                        stop=True,
+                    )
+                if e == 0:
+                    state["y"] = keep.tile([P, N // P, 2 * C], F32, name="y01")
+                if e < 2:
+                    y = state["y"][:, :, e * C : (e + 1) * C]
+                else:
+                    y_tile = small.tile([P, blocks, C], F32, name=f"ysb{i}", tag="ysb")
+                    y = y_tile[:]
+                nc.vector.tensor_tensor(
+                    out=y, in0=acc[:], in1=gate_sb[:, slots].unsqueeze(1).to_broadcast([P, blocks, C]), op=MULT
+                )
+                if e >= 1:
+                    first = 0 if e == 1 else e * C
+                    list_cols = slice(first // 16, (e + 1) * C // 16)
+                    for b in range(blocks):
+                        nb = c0 // P + b
+                        src = state["y"][:, nb, :] if e == 1 else y_tile[:, b, :]
+                        nc.vector.tensor_copy(out=windows[nb][:].indirect(offsets[:, list_cols]), in_=src)
+                        if e == E - 1:
+                            nc.sync.dma_start(out=out[nb * P : (nb + 1) * P, :], in_=windows[nb][:])
+
+        for i in range(AHEAD):
+            load(i)
+            if i == 5:
+                nc.sync.dma_start(gate_sb[:], gate[0:P, :])
+        n = len(chunks)
+        for i in range(n + 2):
+            load(i + AHEAD)
+            if i < n:
+                interleave(i)
+            if 0 <= i - 1 < n:
+                quantize(i - 1)
+            if 0 <= i - 2 < n:
+                after(i - 2)

@@ -28,10 +28,7 @@ def tile_routed_moe_kernel(tc, xT, w1, w3, w2, gate, offs, out):
     with ExitStack() as ctx:
         keep = ctx.enter_context(tc.tile_pool(name="keep", bufs=1))
         raws = ctx.enter_context(tc.tile_pool(name="raws", bufs=AHEAD + 1))
-        stage = ctx.enter_context(tc.tile_pool(name="stage", bufs=6))
-        codes = ctx.enter_context(tc.tile_pool(name="codes", bufs=14))
-        small = ctx.enter_context(tc.tile_pool(name="small", bufs=2))
-        psum = ctx.enter_context(tc.psum_pool(name="psum", bufs=2))
+        psum = ctx.enter_context(tc.psum_pool(name="psum", bufs=1))
 
         offsets = keep.tile([P, E * C // 16], U16, name="offsets")
         nc.sync.dma_start(offsets[:], offs)
@@ -51,6 +48,34 @@ def tile_routed_moe_kernel(tc, xT, w1, w3, w2, gate, offs, out):
             xb = keep.tile([P, T], U8, name=f"x_bytes{g}", align_bytes=64)
             nc.gpsimd.memset(xb[:], 0)
             x_bytes.append(xb)
+        rings = {}
+
+        def ring(kind, count, shape, dtype, pool):
+            tiles = []
+            for r in range(count):
+                if pool is psum:
+                    tiles.append(pool.tile(shape, dtype, name=f"{kind}{r}"))
+                else:
+                    tiles.append(pool.tile(shape, dtype, name=f"{kind}{r}", align_bytes=64))
+            rings[kind] = [tiles, 0]
+
+        def take(kind):
+            tiles, used = rings[kind]
+            rings[kind][1] = used + 1
+            return tiles[used % len(tiles)]
+
+        ring("gv", 2, [P, PACK * H], BF16, keep)
+        ring("gx", PASSES, [P, PACK * H], BF16, keep)
+        ring("gs", 3, [P, PACK * H], BF16, keep)
+        ring("words", 10, [P, H], U32, keep)
+        ring("scales", 10, [P, H], U8, keep)
+        ring("act", 2, [P, PACK, C], F32, keep)
+        ring("hid", 2, [P, C, PACK], BF16, keep)
+        ring("h_words", 2, [P, C], U32, keep)
+        ring("h_bytes", 2, [P, C], U8, keep)
+        ring("a", 2, [P, PACK, C], F32, psum)
+        ring("b", 2, [P, PACK, C], F32, psum)
+        ring("y", 2, [P, PACK, C], F32, psum)
         windows = []
         for nb in range(N // P):
             windows.append(keep.tile([P, T], F32, name=f"window{nb}"))
@@ -98,13 +123,6 @@ def tile_routed_moe_kernel(tc, xT, w1, w3, w2, gate, offs, out):
             kind, e, g, c0, c1 = chunks[i]
             width = c1 - c0
             raw = raw_of[i]
-            grouped = stage.tile([P, PACK * width], BF16, name=f"grouped{i}", tag="grouped", align_bytes=64)
-            if kind in ("w1", "w3"):
-                dst = grouped[:].rearrange("p (t m j) -> p m j t", t=PACK, j=PACK)
-                src = raw[:].rearrange("p j (m t) -> p m j t", t=PACK)
-            else:
-                dst = grouped[:].rearrange("p (c i j) -> p c j i", i=4, j=PACK)
-                src = raw[:].rearrange("p j (c i) -> p c j i", i=4)
             n = width // 4
             if kind == "x":
                 who = "s"
@@ -114,6 +132,13 @@ def tile_routed_moe_kernel(tc, xT, w1, w3, w2, gate, offs, out):
                 who = "s" if c0 == 0 else "b"
             else:
                 who = PLAN[kind][g]
+            grouped = take("gx" if kind == "x" else "gs" if who == "s" else "gv")[:, 0 : PACK * width]
+            if kind in ("w1", "w3"):
+                dst = grouped.rearrange("p (t m j) -> p m j t", t=PACK, j=PACK)
+                src = raw[:].rearrange("p j (m t) -> p m j t", t=PACK)
+            else:
+                dst = grouped.rearrange("p (c i j) -> p c j i", i=4, j=PACK)
+                src = raw[:].rearrange("p j (c i) -> p c j i", i=4)
             if who == "b":
                 cut = (n * 5 // 8) // 8 * 8
                 copy_on("v", dst[:, 0:cut], src[:, 0:cut])
@@ -125,11 +150,10 @@ def tile_routed_moe_kernel(tc, xT, w1, w3, w2, gate, offs, out):
         def quantize(i):
             kind, e, g, c0, c1 = chunks[i]
             if kind == "x":
-                words, scales = x_words[g], x_bytes[g]
+                words, scales = x_words[g][:], x_bytes[g][:]
             else:
-                words = codes.tile([P, c1 - c0], U32, name=f"words{i}", tag="words", align_bytes=64)
-                scales = codes.tile([P, c1 - c0], U8, name=f"scales{i}", tag="scales", align_bytes=64)
-            nc.vector.quantize_mx(out=words[:].bitcast(FP8X4), scales=scales[:], in_=grouped_of[i][:])
+                words, scales = take("words")[:, 0 : c1 - c0], take("scales")[:, 0 : c1 - c0]
+            nc.vector.quantize_mx(out=words.bitcast(FP8X4), scales=scales, in_=grouped_of[i])
             code_of[i] = (words, scales)
 
         def gather(g):
@@ -140,7 +164,7 @@ def tile_routed_moe_kernel(tc, xT, w1, w3, w2, gate, offs, out):
                 nc.vector.tensor_copy(out=xg_bytes[:, g, cols], in_=x_bytes[g][:].indirect(offsets[:, list_cols]))
 
         def first_layer(e, ids, tag):
-            acc = psum.tile([P, PACK, C], F32, name=f"{tag}{e}", tag=tag)
+            acc = take(tag)
             slots = slice(e * C, (e + 1) * C)
             for t in range(PACK):
                 cols = slice(t * P, (t + 1) * P)
@@ -157,79 +181,111 @@ def tile_routed_moe_kernel(tc, xT, w1, w3, w2, gate, offs, out):
                     )
             return acc
 
-        state = {}
+        act_of, hid_of, h_of, a_of, b_of, y_of, ysb_of = {}, {}, {}, {}, {}, {}, {}
 
-        def after(i):
+        def activate(e):
+            act = take("act")
+            nc.scalar.activation(act[:], a_of[e][:], SILU)
+            act_of[e] = act
+
+        def hidden(e):
+            hid = take("hid")
+            nc.vector.tensor_tensor(
+                out=hid[:],
+                in0=b_of[e][:].rearrange("p t c -> p c t"),
+                in1=act_of[e][:].rearrange("p t c -> p c t"),
+                op=MULT,
+            )
+            hid_of[e] = hid
+
+        def quantize_hidden(e):
+            h_words, h_bytes = take("h_words"), take("h_bytes")
+            nc.vector.quantize_mx(
+                out=h_words[:].bitcast(FP8X4), scales=h_bytes[:], in_=hid_of[e][:].rearrange("p c t -> p (c t)")
+            )
+            h_of[e] = (h_words, h_bytes)
+
+        def second_layer(i):
             kind, e, g, c0, c1 = chunks[i]
+            h_words, h_bytes = h_of[e]
+            words, scales = code_of[i]
+            blocks = (c1 - c0) // P
+            acc = take("y")[:, 0:blocks, :]
+            for b in range(blocks):
+                cols = slice(b * P, (b + 1) * P)
+                nc.tensor.matmul_mx(
+                    out=acc[:, b, :],
+                    lhsT=words[:, cols].bitcast(FP8X4),
+                    lhsT_scale=scales[:, cols],
+                    rhs=h_words[:].bitcast(FP8X4),
+                    rhs_scale=h_bytes[:],
+                    start=True,
+                    stop=True,
+                )
+            y_of[i] = acc
+
+        def evacuate(i):
+            kind, e, g, c0, c1 = chunks[i]
+            ysb = take("gv")[:].bitcast(F32)[:, 0 : (c1 - c0) // P * C].rearrange("p (b c) -> p b c", c=C)
+            nc.scalar.copy(ysb, y_of[i])
+            ysb_of[i] = ysb
+
+        def scatter(i, b):
+            kind, e, g, c0, c1 = chunks[i]
+            nb = c0 // P + b
             slots = slice(e * C, (e + 1) * C)
-            if kind == "x":
-                gather(g)
-            elif kind == "w1" and g == PASSES - 1:
-                acc = first_layer(e, (i - 2, i - 1, i), "a")
-                act = small.tile([P, PACK, C], F32, name=f"act{e}", tag="act")
-                nc.scalar.activation(act[:], acc[:], SILU)
-                state["act"] = act
-            elif kind == "w3" and g == PASSES - 1:
-                acc = first_layer(e, (i - 2, i - 1, i), "b")
-                hid = small.tile([P, C, PACK], BF16, name=f"hid{e}", tag="hid", align_bytes=64)
-                nc.vector.tensor_tensor(
-                    out=hid[:],
-                    in0=acc[:].rearrange("p t c -> p c t"),
-                    in1=state["act"][:].rearrange("p t c -> p c t"),
-                    op=MULT,
-                )
-                h_words = small.tile([P, C], U32, name=f"h_words{e}", tag="h_words", align_bytes=64)
-                h_bytes = small.tile([P, C], U8, name=f"h_bytes{e}", tag="h_bytes", align_bytes=64)
-                nc.vector.quantize_mx(
-                    out=h_words[:].bitcast(FP8X4), scales=h_bytes[:], in_=hid[:].rearrange("p c t -> p (c t)")
-                )
-                state["h"] = (h_words, h_bytes)
-            elif kind == "w2":
-                h_words, h_bytes = state["h"]
-                words, scales = code_of[i]
-                blocks = (c1 - c0) // P
-                acc = psum.tile([P, blocks, C], F32, name=f"y{i}", tag="y")
-                for b in range(blocks):
-                    cols = slice(b * P, (b + 1) * P)
-                    nc.tensor.matmul_mx(
-                        out=acc[:, b, :],
-                        lhsT=words[:, cols].bitcast(FP8X4),
-                        lhsT_scale=scales[:, cols],
-                        rhs=h_words[:].bitcast(FP8X4),
-                        rhs_scale=h_bytes[:],
-                        start=True,
-                        stop=True,
-                    )
-                if e == 0:
-                    state["y"] = keep.tile([P, N // P, 2 * C], F32, name="y01")
-                if e < 2:
-                    y = state["y"][:, :, e * C : (e + 1) * C]
-                else:
-                    y_tile = small.tile([P, blocks, C], F32, name=f"ysb{i}", tag="ysb")
-                    y = y_tile[:]
-                nc.vector.tensor_tensor(
-                    out=y, in0=acc[:], in1=gate_sb[:, slots].unsqueeze(1).to_broadcast([P, blocks, C]), op=MULT
-                )
-                if e >= 1:
-                    first = 0 if e == 1 else e * C
-                    list_cols = slice(first // 16, (e + 1) * C // 16)
-                    for b in range(blocks):
-                        nb = c0 // P + b
-                        src = state["y"][:, nb, :] if e == 1 else y_tile[:, b, :]
-                        nc.vector.tensor_copy(out=windows[nb][:].indirect(offsets[:, list_cols]), in_=src)
-                        if e == E - 1:
-                            nc.sync.dma_start(out=out[nb * P : (nb + 1) * P, :], in_=windows[nb][:])
+            list_cols = slice(e * C // 16, (e + 1) * C // 16)
+            nc.vector.tensor_tensor(
+                out=windows[nb][:].indirect(offsets[:, list_cols]), in0=ysb_of[i][:, b, :], in1=gate_sb[:, slots], op=MULT
+            )
+            if e == E - 1:
+                nc.sync.dma_start(out=out[nb * P : (nb + 1) * P, :], in_=windows[nb][:])
+
+        def act_a(e, i):
+            a_of[e] = first_layer(e, (i - 2, i - 1, i), "a")
+
+        def act_b(e, i):
+            b_of[e] = first_layer(e, (i - 2, i - 1, i), "b")
 
         for i in range(AHEAD):
             load(i)
             if i == 5:
                 nc.sync.dma_start(gate_sb[:], gate[0:P, :])
         n = len(chunks)
-        for i in range(n + 2):
+        tasks = {}
+
+        def at(step, fn, *args):
+            tasks.setdefault(step, []).append((fn, args))
+
+        first_tasks = {}
+
+        def before(step, fn, *args):
+            first_tasks.setdefault(step, []).append((fn, args))
+
+        for i in range(n):
+            kind, e, g, c0, c1 = chunks[i]
+            if kind == "x":
+                at(i + 2, gather, g)
+            elif kind == "w1" and g == PASSES - 1:
+                at(i + 1, act_a, e, i)
+                at(i + 2, activate, e)
+            elif kind == "w3" and g == PASSES - 1:
+                at(i + 1, act_b, e, i)
+                at(i + 2, hidden, e)
+                before(i + 3, quantize_hidden, e)
+            elif kind == "w2":
+                at(i + 2, second_layer, i)
+                at(i + 2, evacuate, i)
+                blocks = (c1 - c0) // P
+                for b in range(blocks):
+                    at(i + 3 + b // 2, scatter, i, b)
+        for i in range(n + 12):
             load(i + AHEAD)
+            for fn, args in first_tasks.get(i, []):
+                fn(*args)
             if i < n:
                 interleave(i)
             if 0 <= i - 1 < n:
                 quantize(i - 1)
-            if 0 <= i - 2 < n:
-                after(i - 2)
+            for fn, args in tasks.get(i, []):
+                fn(*args)

@@ -20,7 +20,7 @@ FP8X4 = mybir.dt.float8_e4m3fn_x4
 MULT = mybir.AluOpType.mult
 SILU = mybir.ActivationFunctionType.Silu
 
-AHEAD = 13
+AHEAD = 10
 
 
 def tile_routed_moe_kernel(tc, xT, w1, w3, w2, gate, offs, out):
@@ -65,17 +65,21 @@ def tile_routed_moe_kernel(tc, xT, w1, w3, w2, gate, offs, out):
             return tiles[used % len(tiles)]
 
         ring("gv", 2, [P, PACK * H], BF16, keep)
+        ring("pair", 3, [P, 2 * PACK * H], BF16, keep)
+        ring("pair_words", 6, [P, 2 * H], U32, keep)
+        ring("pair_scales", 6, [P, 2 * H], U8, keep)
+        ring("ysb", 2, [P, N // P, C], F32, keep)
         ring("gx", PASSES, [P, PACK * H], BF16, keep)
-        ring("gs", 3, [P, PACK * H], BF16, keep)
-        ring("words", 10, [P, H], U32, keep)
-        ring("scales", 10, [P, H], U8, keep)
+        ring("gs", 2, [P, PACK * H], BF16, keep)
+        ring("words", 8, [P, H], U32, keep)
+        ring("scales", 8, [P, H], U8, keep)
         ring("act", 2, [P, PACK, C], F32, keep)
         ring("hid", 2, [P, C, PACK], BF16, keep)
         ring("h_words", 2, [P, C], U32, keep)
         ring("h_bytes", 2, [P, C], U8, keep)
         ring("a", 2, [P, PACK, C], F32, psum)
         ring("b", 2, [P, PACK, C], F32, psum)
-        ring("y", 2, [P, PACK, C], F32, psum)
+        ring("y", 3, [P, N // P, C], F32, psum)
         windows = []
         for nb in range(N // P):
             windows.append(keep.tile([P, T], F32, name=f"window{nb}"))
@@ -86,11 +90,7 @@ def tile_routed_moe_kernel(tc, xT, w1, w3, w2, gate, offs, out):
                 chunks.append(("w1", e, g, 0, H))
             for g in range(PASSES):
                 chunks.append(("w3", e, g, 0, H))
-            if e < E - 1:
-                chunks.append(("w2", e, 0, 0, N))
-            else:
-                chunks.append(("w2", e, 0, 0, N // 2))
-                chunks.append(("w2", e, 0, N // 2, N))
+            chunks.append(("w2", e, 0, 0, N))
 
         raw_of, grouped_of, code_of = {}, {}, {}
 
@@ -117,22 +117,24 @@ def tile_routed_moe_kernel(tc, xT, w1, w3, w2, gate, offs, out):
             else:
                 nc.scalar.copy(out_, in_)
 
-        PLAN = {"w1": "svs", "w3": "ssv", "w2": "s"}
+        PLAN = "vss" + "vsvssvs" + "svsssvs" + "svsssvs" + "sbssbbb"
+
+        first_of_pair = [3 + 7 * e + 2 * r for e in range(E - 1) for r in range(3)]
+        pair_tile = {}
 
         def interleave(i):
             kind, e, g, c0, c1 = chunks[i]
             width = c1 - c0
             raw = raw_of[i]
             n = width // 4
-            if kind == "x":
-                who = "s"
-            elif kind == "w3" and e == E - 1 and g == PASSES - 1:
-                who = "b"
-            elif kind == "w2" and e == E - 1:
-                who = "s" if c0 == 0 else "b"
+            who = PLAN[i]
+            if i in first_of_pair:
+                pair_tile[i] = take("pair")
+                grouped = pair_tile[i][:, 0 : PACK * H]
+            elif i - 1 in first_of_pair:
+                grouped = pair_tile[i - 1][:, PACK * H :]
             else:
-                who = PLAN[kind][g]
-            grouped = take("gx" if kind == "x" else "gs" if who == "s" else "gv")[:, 0 : PACK * width]
+                grouped = take("gx" if kind == "x" else "gs" if who == "s" else "gv")[:]
             if kind in ("w1", "w3"):
                 dst = grouped.rearrange("p (t m j) -> p m j t", t=PACK, j=PACK)
                 src = raw[:].rearrange("p j (m t) -> p m j t", t=PACK)
@@ -149,12 +151,20 @@ def tile_routed_moe_kernel(tc, xT, w1, w3, w2, gate, offs, out):
 
         def quantize(i):
             kind, e, g, c0, c1 = chunks[i]
+            if i in first_of_pair:
+                return
+            if i - 1 in first_of_pair:
+                words, scales = take("pair_words"), take("pair_scales")
+                nc.vector.quantize_mx(out=words[:].bitcast(FP8X4), scales=scales[:], in_=pair_tile[i - 1][:])
+                code_of[i - 1] = (words[:, 0:H], scales[:, 0:H])
+                code_of[i] = (words[:, H:], scales[:, H:])
+                return
             if kind == "x":
-                words, scales = x_words[g][:], x_bytes[g][:]
+                words, scales = x_words[g], x_bytes[g]
             else:
-                words, scales = take("words")[:, 0 : c1 - c0], take("scales")[:, 0 : c1 - c0]
-            nc.vector.quantize_mx(out=words.bitcast(FP8X4), scales=scales, in_=grouped_of[i])
-            code_of[i] = (words, scales)
+                words, scales = take("words"), take("scales")
+            nc.vector.quantize_mx(out=words[:].bitcast(FP8X4), scales=scales[:], in_=grouped_of[i])
+            code_of[i] = (words[:], scales[:])
 
         def gather(g):
             for h in range(2):
@@ -205,16 +215,15 @@ def tile_routed_moe_kernel(tc, xT, w1, w3, w2, gate, offs, out):
             )
             h_of[e] = (h_words, h_bytes)
 
-        def second_layer(i):
-            kind, e, g, c0, c1 = chunks[i]
+        def second_layer(i, first, blocks):
+            e = chunks[i][1]
             h_words, h_bytes = h_of[e]
             words, scales = code_of[i]
-            blocks = (c1 - c0) // P
-            acc = take("y")[:, 0:blocks, :]
-            for b in range(blocks):
+            acc = take("y")
+            for b in range(first, first + blocks):
                 cols = slice(b * P, (b + 1) * P)
                 nc.tensor.matmul_mx(
-                    out=acc[:, b, :],
+                    out=acc[:, b - first, :],
                     lhsT=words[:, cols].bitcast(FP8X4),
                     lhsT_scale=scales[:, cols],
                     rhs=h_words[:].bitcast(FP8X4),
@@ -222,21 +231,22 @@ def tile_routed_moe_kernel(tc, xT, w1, w3, w2, gate, offs, out):
                     start=True,
                     stop=True,
                 )
-            y_of[i] = acc
+            y_of[i, first] = acc
 
-        def evacuate(i):
-            kind, e, g, c0, c1 = chunks[i]
-            ysb = take("gv")[:].bitcast(F32)[:, 0 : (c1 - c0) // P * C].rearrange("p (b c) -> p b c", c=C)
-            nc.scalar.copy(ysb, y_of[i])
-            ysb_of[i] = ysb
+        def evacuate(i, first, blocks):
+            ysb = take("ysb")[:, 0:blocks, :]
+            nc.scalar.copy(ysb, y_of[i, first][:, 0:blocks, :])
+            ysb_of[i, first] = ysb
 
-        def scatter(i, b):
-            kind, e, g, c0, c1 = chunks[i]
-            nb = c0 // P + b
+        def scatter(i, first, nb):
+            e = chunks[i][1]
             slots = slice(e * C, (e + 1) * C)
             list_cols = slice(e * C // 16, (e + 1) * C // 16)
             nc.vector.tensor_tensor(
-                out=windows[nb][:].indirect(offsets[:, list_cols]), in0=ysb_of[i][:, b, :], in1=gate_sb[:, slots], op=MULT
+                out=windows[nb][:].indirect(offsets[:, list_cols]),
+                in0=ysb_of[i, first][:, nb - first, :],
+                in1=gate_sb[:, slots],
+                op=MULT,
             )
             if e == E - 1:
                 nc.sync.dma_start(out=out[nb * P : (nb + 1) * P, :], in_=windows[nb][:])
@@ -267,18 +277,20 @@ def tile_routed_moe_kernel(tc, xT, w1, w3, w2, gate, offs, out):
             if kind == "x":
                 at(i + 2, gather, g)
             elif kind == "w1" and g == PASSES - 1:
-                at(i + 1, act_a, e, i)
-                at(i + 2, activate, e)
+                late = 1 if i in first_of_pair else 0
+                at(i + 1 + late, act_a, e, i)
+                at(i + 2 + late, activate, e)
             elif kind == "w3" and g == PASSES - 1:
                 at(i + 1, act_b, e, i)
                 at(i + 2, hidden, e)
                 before(i + 3, quantize_hidden, e)
             elif kind == "w2":
-                at(i + 2, second_layer, i)
-                at(i + 2, evacuate, i)
-                blocks = (c1 - c0) // P
-                for b in range(blocks):
-                    at(i + 3 + b // 2, scatter, i, b)
+                blocks = 2 if e == E - 1 else 4
+                for first in range(0, N // P, blocks):
+                    at(i + 2, second_layer, i, first, blocks)
+                    at(i + 2, evacuate, i, first, blocks)
+                for nb in range(N // P):
+                    at(i + 3 + nb // 2, scatter, i, nb // blocks * blocks, nb)
         for i in range(n + 12):
             load(i + AHEAD)
             for fn, args in first_tasks.get(i, []):

@@ -9,7 +9,7 @@ K_PASS = P * PACK
 PASSES = K // K_PASS
 
 FLOPS = 2 * E * C * (K * H * 2 + H * N)
-BYTES = 4 * (K * T + 2 * E * K * H + E * H * N + P * E * C + N * T) + 2 * P * E * C // 16
+BYTES = 4 * (K * T + 2 * E * K * H + E * H * N + E * C + N * T) + 2 * P * E * C // 16
 
 F32 = mybir.dt.float32
 BF16 = mybir.dt.bfloat16
@@ -39,6 +39,11 @@ def tile_routed_moe_kernel(tc, xT, w1, w3, w2, gate, offs, out):
         nc.scalar.activation(warm_out[:], warm[:], SILU)
 
         gate_sb = keep.tile([P, E * C], F32, name="gate_sb")
+        gate_row = keep.tile([P, E * C], F32, name="gate_row")
+        ones = keep.tile([P, P], F32, name="ones")
+        nc.gpsimd.memset(gate_row[:], 0.0)
+        nc.gpsimd.memset(ones[:], 1.0)
+        gate_psum = psum.tile([P, E * C], F32, name="gate_psum")
         xg_words = keep.tile([P, PASSES, E * C], U32, name="xg_words", align_bytes=64)
         xg_bytes = keep.tile([P, PASSES, E * C], U8, name="xg_bytes", align_bytes=64)
         x_words = []
@@ -117,7 +122,7 @@ def tile_routed_moe_kernel(tc, xT, w1, w3, w2, gate, offs, out):
             else:
                 nc.scalar.copy(out_, in_)
 
-        PLAN = "vss" + "vsvssvs" + "svsssvs" + "svsssvs" + "sbssbbb"
+        PLAN = "vss" + "vsvssvs" + "svsssvs" + "svsssvs" + "sbssbtb"
 
         first_of_pair = [3 + 7 * e + 2 * r for e in range(E - 1) for r in range(3)]
         pair_tile = {}
@@ -141,7 +146,10 @@ def tile_routed_moe_kernel(tc, xT, w1, w3, w2, gate, offs, out):
             else:
                 dst = grouped.rearrange("p (c i j) -> p c j i", i=4, j=PACK)
                 src = raw[:].rearrange("p j (c i) -> p c j i", i=4)
-            if who == "b":
+            if who == "t":
+                copy_on("v", dst[:, :, :, 0:2], src[:, :, :, 0:2])
+                copy_on("s", dst[:, :, :, 2:4], src[:, :, :, 2:4])
+            elif who == "b":
                 cut = (n * 5 // 8) // 8 * 8
                 copy_on("v", dst[:, 0:cut], src[:, 0:cut])
                 copy_on("s", dst[:, cut:n], src[:, cut:n])
@@ -163,7 +171,14 @@ def tile_routed_moe_kernel(tc, xT, w1, w3, w2, gate, offs, out):
                 words, scales = x_words[g], x_bytes[g]
             else:
                 words, scales = take("words"), take("scales")
-            nc.vector.quantize_mx(out=words[:].bitcast(FP8X4), scales=scales[:], in_=grouped_of[i])
+            parts = 2 if PLAN[i] == "t" else 1
+            for r in range(parts):
+                cols = slice(r * H // parts, (r + 1) * H // parts)
+                nc.vector.quantize_mx(
+                    out=words[:, cols].bitcast(FP8X4),
+                    scales=scales[:, cols],
+                    in_=grouped_of[i][:, PACK * cols.start : PACK * cols.stop],
+                )
             code_of[i] = (words[:], scales[:])
 
         def gather(g):
@@ -260,7 +275,8 @@ def tile_routed_moe_kernel(tc, xT, w1, w3, w2, gate, offs, out):
         for i in range(AHEAD):
             load(i)
             if i == 5:
-                nc.sync.dma_start(gate_sb[:], gate[0:P, :])
+                nc.sync.dma_start(gate_row[0:1, :], gate[0:1, :])
+                nc.tensor.matmul(gate_psum[:], lhsT=ones[:], rhs=gate_row[:], start=True, stop=True)
         n = len(chunks)
         tasks = {}
 
@@ -291,6 +307,7 @@ def tile_routed_moe_kernel(tc, xT, w1, w3, w2, gate, offs, out):
                     at(i + 2, evacuate, i, first, blocks)
                 for nb in range(N // P):
                     at(i + 3 + nb // 2, scatter, i, nb // blocks * blocks, nb)
+        at(7, nc.scalar.copy, gate_sb[:], gate_psum[:])
         for i in range(n + 12):
             load(i + AHEAD)
             for fn, args in first_tasks.get(i, []):

from contextlib import ExitStack

import concourse.mybir as mybir

K, T, E, C, H, N = 1536, 512, 4, 128, 512, 512
P = 128
PACK = 4
K_PASS = P * PACK
PASSES = K // K_PASS

FLOPS = 2 * E * C * (K * H * 2 + H * N)
BYTES = 4 * (K * T + 2 * E * K * H + E * H * N + E * C + N * T) + 2 * P * E * C // 16

F32 = mybir.dt.float32
BF16 = mybir.dt.bfloat16
U32 = mybir.dt.uint32
U16 = mybir.dt.uint16
U8 = mybir.dt.uint8
FP8X4 = mybir.dt.float8_e4m3fn_x4
MULT = mybir.AluOpType.mult
SILU = mybir.ActivationFunctionType.Silu

AHEAD = 10


def tile_routed_moe_kernel(tc, xT, w1, w3, w2, gate, offs, out):
    nc = tc.nc
    with ExitStack() as ctx:
        keep = ctx.enter_context(tc.tile_pool(name="keep", bufs=1))
        raws = ctx.enter_context(tc.tile_pool(name="raws", bufs=AHEAD + 1))
        psum = ctx.enter_context(tc.psum_pool(name="psum", bufs=1))

        offsets = keep.tile([P, E * C // 16], U16, name="offsets")
        nc.sync.dma_start(offsets[:], offs)

        warm = keep.tile([P, 1], F32, name="warm")
        warm_out = keep.tile([P, 1], F32, name="warm_out")
        nc.vector.memset(warm[:], 0.0)
        nc.scalar.activation(warm_out[:], warm[:], SILU)

        gate_sb = keep.tile([P, E * C], F32, name="gate_sb")
        gate_row = keep.tile([P, E * C], F32, name="gate_row")
        ones = keep.tile([P, P], F32, name="ones")
        nc.gpsimd.memset(gate_row[:], 0.0)
        nc.gpsimd.memset(ones[:], 1.0)
        gate_psum = psum.tile([P, E * C], F32, name="gate_psum")
        xg_words = keep.tile([P, PASSES, E * C], U32, name="xg_words", align_bytes=64)
        xg_bytes = keep.tile([P, PASSES, E * C], U8, name="xg_bytes", align_bytes=64)
        x_words = []
        x_bytes = []
        for g in range(PASSES):
            x_words.append(keep.tile([P, T], U32, name=f"x_words{g}", align_bytes=64))
            xb = keep.tile([P, T], U8, name=f"x_bytes{g}", align_bytes=64)
            nc.gpsimd.memset(xb[:], 0)
            x_bytes.append(xb)
        rings = {}

        def ring(kind, count, shape, dtype, pool):
            tiles = []
            for r in range(count):
                if pool is psum:
                    tiles.append(pool.tile(shape, dtype, name=f"{kind}{r}"))
                else:
                    tiles.append(pool.tile(shape, dtype, name=f"{kind}{r}", align_bytes=64))
            rings[kind] = [tiles, 0]

        def take(kind):
            tiles, used = rings[kind]
            rings[kind][1] = used + 1
            return tiles[used % len(tiles)]

        ring("gv", 2, [P, PACK * H], BF16, keep)
        ring("pair", 3, [P, 2 * PACK * H], BF16, keep)
        ring("pair_words", 6, [P, 2 * H], U32, keep)
        ring("pair_scales", 6, [P, 2 * H], U8, keep)
        ring("ysb", 2, [P, N // P, C], F32, keep)
        ring("gx", PASSES, [P, PACK * H], BF16, keep)
        ring("gs", 2, [P, PACK * H], BF16, keep)
        ring("words", 8, [P, H], U32, keep)
        ring("scales", 8, [P, H], U8, keep)
        ring("act", 2, [P, PACK, C], F32, keep)
        ring("hid", 2, [P, C, PACK], BF16, keep)
        ring("h_words", 2, [P, C], U32, keep)
        ring("h_bytes", 2, [P, C], U8, keep)
        ring("a", 2, [P, PACK, C], F32, psum)
        ring("b", 2, [P, PACK, C], F32, psum)
        ring("y", 3, [P, N // P, C], F32, psum)
        windows = []
        for nb in range(N // P):
            windows.append(keep.tile([P, T], F32, name=f"window{nb}"))

        chunks = [("x", 0, g, 0, T) for g in range(PASSES)]
        for e in range(E):
            for g in range(PASSES):
                chunks.append(("w1", e, g, 0, H))
            for g in range(PASSES):
                chunks.append(("w3", e, g, 0, H))
            chunks.append(("w2", e, 0, 0, N))

        raw_of, grouped_of, code_of = {}, {}, {}

        def load(i):
            if i >= len(chunks):
                return
            kind, e, g, c0, c1 = chunks[i]
            rows = slice(g * K_PASS, (g + 1) * K_PASS)
            if kind == "x":
                src = xT[rows, :]
            elif kind == "w1":
                src = w1[e, rows, :]
            elif kind == "w3":
                src = w3[e, rows, :]
            else:
                src = w2[e, :, c0:c1]
            raw = raws.tile([P, PACK, c1 - c0], F32, name=f"raw{i}", tag="raw")
            nc.sync.dma_start(out=raw[:], in_=src.rearrange("(p j) w -> p j w", j=PACK))
            raw_of[i] = raw

        def copy_on(engine, out_, in_):
            if engine == "v":
                nc.vector.tensor_copy(out=out_, in_=in_)
            else:
                nc.scalar.copy(out_, in_)

        PLAN = "vss" + "vsvssvs" + "svsssvs" + "svsssvs" + "sbssbtb"

        first_of_pair = [3 + 7 * e + 2 * r for e in range(E - 1) for r in range(3)]
        pair_tile = {}

        def interleave(i):
            kind, e, g, c0, c1 = chunks[i]
            width = c1 - c0
            raw = raw_of[i]
            n = width // 4
            who = PLAN[i]
            if i in first_of_pair:
                pair_tile[i] = take("pair")
                grouped = pair_tile[i][:, 0 : PACK * H]
            elif i - 1 in first_of_pair:
                grouped = pair_tile[i - 1][:, PACK * H :]
            else:
                grouped = take("gx" if kind == "x" else "gs" if who == "s" else "gv")[:]
            if kind in ("w1", "w3"):
                dst = grouped.rearrange("p (t m j) -> p m j t", t=PACK, j=PACK)
                src = raw[:].rearrange("p j (m t) -> p m j t", t=PACK)
            else:
                dst = grouped.rearrange("p (c i j) -> p c j i", i=4, j=PACK)
                src = raw[:].rearrange("p j (c i) -> p c j i", i=4)
            if who == "t":
                copy_on("v", dst[:, :, :, 0:2], src[:, :, :, 0:2])
                copy_on("s", dst[:, :, :, 2:4], src[:, :, :, 2:4])
            elif who == "b":
                cut = (n * 5 // 8) // 8 * 8
                copy_on("v", dst[:, 0:cut], src[:, 0:cut])
                copy_on("s", dst[:, cut:n], src[:, cut:n])
            else:
                copy_on(who, dst, src)
            grouped_of[i] = grouped

        def quantize(i):
            kind, e, g, c0, c1 = chunks[i]
            if i in first_of_pair:
                return
            if i - 1 in first_of_pair:
                words, scales = take("pair_words"), take("pair_scales")
                nc.vector.quantize_mx(out=words[:].bitcast(FP8X4), scales=scales[:], in_=pair_tile[i - 1][:])
                code_of[i - 1] = (words[:, 0:H], scales[:, 0:H])
                code_of[i] = (words[:, H:], scales[:, H:])
                return
            if kind == "x":
                words, scales = x_words[g], x_bytes[g]
            else:
                words, scales = take("words"), take("scales")
            parts = 2 if PLAN[i] == "t" else 1
            for r in range(parts):
                cols = slice(r * H // parts, (r + 1) * H // parts)
                nc.vector.quantize_mx(
                    out=words[:, cols].bitcast(FP8X4),
                    scales=scales[:, cols],
                    in_=grouped_of[i][:, PACK * cols.start : PACK * cols.stop],
                )
            code_of[i] = (words[:], scales[:])

        def gather(g):
            for h in range(2):
                cols = slice(h * 256, (h + 1) * 256)
                list_cols = slice(h * 16, (h + 1) * 16)
                nc.vector.tensor_copy(out=xg_words[:, g, cols], in_=x_words[g][:].indirect(offsets[:, list_cols]))
                nc.vector.tensor_copy(out=xg_bytes[:, g, cols], in_=x_bytes[g][:].indirect(offsets[:, list_cols]))

        def first_layer(e, ids, tag):
            acc = take(tag)
            slots = slice(e * C, (e + 1) * C)
            for t in range(PACK):
                cols = slice(t * P, (t + 1) * P)
                for g in range(PASSES):
                    words, scales = code_of[ids[g]]
                    nc.tensor.matmul_mx(
                        out=acc[:, t, :],
                        lhsT=words[:, cols].bitcast(FP8X4),
                        lhsT_scale=scales[:, cols],
                        rhs=xg_words[:, g, slots].bitcast(FP8X4),
                        rhs_scale=xg_bytes[:, g, slots],
                        start=(g == 0),
                        stop=(g == PASSES - 1),
                    )
            return acc

        act_of, hid_of, h_of, a_of, b_of, y_of, ysb_of = {}, {}, {}, {}, {}, {}, {}

        def activate(e):
            act = take("act")
            nc.scalar.activation(act[:], a_of[e][:], SILU)
            act_of[e] = act

        def hidden(e):
            hid = take("hid")
            nc.vector.tensor_tensor(
                out=hid[:],
                in0=b_of[e][:].rearrange("p t c -> p c t"),
                in1=act_of[e][:].rearrange("p t c -> p c t"),
                op=MULT,
            )
            hid_of[e] = hid

        def quantize_hidden(e):
            h_words, h_bytes = take("h_words"), take("h_bytes")
            nc.vector.quantize_mx(
                out=h_words[:].bitcast(FP8X4), scales=h_bytes[:], in_=hid_of[e][:].rearrange("p c t -> p (c t)")
            )
            h_of[e] = (h_words, h_bytes)

        def second_layer(i, first, blocks):
            e = chunks[i][1]
            h_words, h_bytes = h_of[e]
            words, scales = code_of[i]
            acc = take("y")
            for b in range(first, first + blocks):
                cols = slice(b * P, (b + 1) * P)
                nc.tensor.matmul_mx(
                    out=acc[:, b - first, :],
                    lhsT=words[:, cols].bitcast(FP8X4),
                    lhsT_scale=scales[:, cols],
                    rhs=h_words[:].bitcast(FP8X4),
                    rhs_scale=h_bytes[:],
                    start=True,
                    stop=True,
                )
            y_of[i, first] = acc

        def evacuate(i, first, blocks):
            ysb = take("ysb")[:, 0:blocks, :]
            nc.scalar.copy(ysb, y_of[i, first][:, 0:blocks, :])
            ysb_of[i, first] = ysb

        def scatter(i, first, nb):
            e = chunks[i][1]
            slots = slice(e * C, (e + 1) * C)
            list_cols = slice(e * C // 16, (e + 1) * C // 16)
            nc.vector.tensor_tensor(
                out=windows[nb][:].indirect(offsets[:, list_cols]),
                in0=ysb_of[i, first][:, nb - first, :],
                in1=gate_sb[:, slots],
                op=MULT,
            )
            if e == E - 1:
                nc.sync.dma_start(out=out[nb * P : (nb + 1) * P, :], in_=windows[nb][:])

        def act_a(e, i):
            a_of[e] = first_layer(e, (i - 2, i - 1, i), "a")

        def act_b(e, i):
            b_of[e] = first_layer(e, (i - 2, i - 1, i), "b")

        for i in range(AHEAD):
            load(i)
            if i == 5:
                nc.sync.dma_start(gate_row[0:1, :], gate[0:1, :])
                nc.tensor.matmul(gate_psum[:], lhsT=ones[:], rhs=gate_row[:], start=True, stop=True)
        n = len(chunks)
        tasks = {}

        def at(step, fn, *args):
            tasks.setdefault(step, []).append((fn, args))

        first_tasks = {}

        def before(step, fn, *args):
            first_tasks.setdefault(step, []).append((fn, args))

        for i in range(n):
            kind, e, g, c0, c1 = chunks[i]
            if kind == "x":
                at(i + 2, gather, g)
            elif kind == "w1" and g == PASSES - 1:
                late = 1 if i in first_of_pair else 0
                at(i + 1 + late, act_a, e, i)
                at(i + 2 + late, activate, e)
            elif kind == "w3" and g == PASSES - 1:
                at(i + 1, act_b, e, i)
                at(i + 2, hidden, e)
                before(i + 3, quantize_hidden, e)
            elif kind == "w2":
                blocks = 2 if e == E - 1 else 4
                for first in range(0, N // P, blocks):
                    at(i + 2, second_layer, i, first, blocks)
                    at(i + 2, evacuate, i, first, blocks)
                for nb in range(N // P):
                    at(i + 3 + nb // 2, scatter, i, nb // blocks * blocks, nb)
        at(7, nc.scalar.copy, gate_sb[:], gate_psum[:])
        for i in range(n + 12):
            load(i + AHEAD)
            for fn, args in first_tasks.get(i, []):
                fn(*args)
            if i < n:
                interleave(i)
            if 0 <= i - 1 < n:
                quantize(i - 1)
            for fn, args in tasks.get(i, []):
                fn(*args)
